import numpy as np, ml_dtypes
CORES = [120,124,248,252,376,380,504,508]
N = 8
import mx_ref
NC, ROOT = 128, 4
BF = ml_dtypes.bfloat16
def cut(t, i, w=512):
    return t[:, w * i:w * i + w]
def term(a, B):
    return np.stack([np.maximum(mx_ref.matmul(mx_ref.quantize(cut(a, i)), B), 0) for i in range(4)], axis=2).reshape(128, -1)
def setup_inputs(rng):
    def f(*shape):
        return mx_ref.flush((rng.standard_normal(shape, dtype=np.float32) * np.exp2(rng.integers(-2, 3, shape[:-1] + (1,)))).astype(BF))
    return {"a": f(N, 128, 4 * 512), "b": f(N, 128, 4 * NC)}
def setup_inputs_blocks(rng):
    d = setup_inputs(rng)
    for k in ("a", "b"): d[k] = mx_ref.spread(d[k], rng, 2)
    return d
def setup_inputs_wide(rng):
    d = setup_inputs(rng)
    for k in ("a", "b"): d[k] = mx_ref.flush((d[k].astype(np.float32) * np.exp2(rng.integers(-4, 5, (N, 1, 1))).astype(np.float32)).astype(BF))
    return d
def setup_inputs_lossless(rng):
    a = np.zeros((N, 128, 4 * 128, 4), np.float32)
    for r in range(N):
        k = rng.integers(0, 512, size=4 * 128)
        a[r, k // 4, np.arange(4 * 128), k % 4] = 1.0
    size = np.repeat(2.0 ** rng.integers(-4, 5, size=(1, 1, (4 * NC) // 4)), 4, axis=2)
    b = (rng.random((N, 128, 4 * NC)) < 0.8) * size
    return {"a": a.reshape(N, 128, 4 * 512).astype(BF), "b": b.astype(np.float32).astype(BF)}
def reference(a, b):
    B0 = mx_ref.quantize(b[ROOT])
    T = [term(a[r], B0) for r in range(N)]
    y = np.zeros((N, 128, 4 * NC), np.float32)
    y[:] = mx_ref.total(T)
    return {"y": y}

@@ -1,0 +1,234 @@
+from concourse.bass import DstId, RemoteDMATransfer
+from concourse.mybir import dt, AluOpType, ActivationFunctionType
+
+NC = 128
+HALF = NC // 2
+BANK = 512
+
+F8, U8 = "float8_e4m3fn_x4", "uint8"
+SCRATCH = {
+    "a_sb": ("sbuf", [128, 2048], "bfloat16"),
+    "b_sb": ("sbuf", [128, 512], "bfloat16"),
+    "sel": ("sbuf", [128, 516], "bfloat16"),
+    "e1": ("sbuf", [128, 512], "bfloat16"),
+    "e1f": ("sbuf", [128, 512], "float32"),
+    "e2": ("sbuf", [128, 512], "bfloat16"),
+    "y_sb": ("sbuf", [128, 512], "float32"),
+    "aq": ("sbuf", [128, 512], F8), "aqs": ("sbuf", [128, 512], U8),
+    "bq": ("sbuf", [128, 128], F8), "bqs": ("sbuf", [128, 128], U8),
+    "sq": ("sbuf", [128, 512], F8), "sqs": ("sbuf", [128, 512], U8),
+    "gt": ("sbuf", [128, 128], F8), "gts": ("sbuf", [128, 128], U8),
+    "l1": ("sbuf", [128, 320], F8), "l1s": ("sbuf", [128, 320], U8),
+    "qa": ("sbuf", [128, 192], F8), "qas": ("sbuf", [128, 192], U8),
+    "fb": ("sbuf", [128, 128], F8), "fbs": ("sbuf", [128, 128], U8),
+    "pt": ("psum", [128, 2048], "float32"),
+    "ps": ("psum", [128, 2048], "float32"),
+}
+SEMAPHORES = (["ld_a", "ld_b", "ones", "seld", "e2z", "aqd", "bqd", "sqd", "rv", "rs", "av", "qt", "cv", "cs", "qad", "yv", "ys",
+               "out", "sent", "ing", "fa", "fb0", "fb1", "in0", "in1", "in2"]
+              + [k + str(i) for k in "mgdf" for i in range(4)])
+
+
+def _engines(mask):
+    return [e for e in range(16) if mask >> e & 1]
+
+
+def _bits(engines):
+    m = 0
+    for e in engines:
+        m |= 1 << e
+    return m
+
+
+def _plan(T, topo):
+    cs = list(T.cores)
+    pick = lambda l, c, same: [d for d in l if (topo.die(d) == topo.die(c)) == same][0]
+    near = {}
+    for c in cs:
+        chip = [d for d in cs if d != c and topo.host(d) == topo.host(c) and topo.chip(d) == topo.chip(c)]
+        plane = [d for d in cs if topo.same_plane(c, d)]
+        cable = [d for d in cs if topo.rack(topo.host(d)) != topo.rack(topo.host(c)) and topo.may_write(c, d)]
+        near[c] = {"mate": chip[0], "plane": pick(plane, c, True), "plane_x": pick(plane, c, False),
+                   "cable": pick(cable, c, True), "cable_x": pick(cable, c, False)}
+    root = cs[T.root]
+    x, w = near[root]["cable"], near[root]["plane"]
+    tree = {root: [x, w, near[root]["mate"]], x: [near[x]["plane"], near[x]["mate"]], w: [near[w]["cable_x"], near[w]["mate"]]}
+    depth = {root: 0}
+    for c in (root, x, w):
+        for d in tree[c]:
+            depth[d] = depth[c] + 1
+    src = {c: sorted([d for d in (near[c]["mate"], near[c]["plane"], near[c]["plane_x"]) if d != root],
+                     key=lambda d: depth[d]) for c in cs}
+    return near, root, tree, src
+
+
+def rank_program(g, core, T, topo):
+    if T.rank_of(core) is None:
+        return
+    near, root, tree, src = _plan(T, topo)
+    me = near[core]
+    is_root, is_agg = core == root, me["mate"] == root
+
+    def half(c):
+        return topo.die(c)
+
+    def split(c, dests):
+        mate = near[c]["mate"]
+        off = [d for d in dests if d != mate]
+        eng = _engines(topo.mask(c, near[c]["plane"]))
+        k = len(eng) // max(len(off), 1 if off else 2)
+        out = {d: eng[i * k:(i + 1) * k] for i, d in enumerate(off)}
+        if mate in dests:
+            out[mate] = [e for e in _engines(topo.mask(c, mate)) if e not in eng][:k]
+        return out
+
+    sent = [0]
+
+    def send(items):
+        eng = split(core, [it[0] for it in items])
+        for codes in (True, False):
+            trs = []
+            for d, sn, a, n, dn, b, sem in items:
+                rid, pid = topo.addr(d, core)
+                if codes:
+                    s, t = T[sn][:, a:a + n].bitcast(dt.uint8), T[dn][:, b:b + n].bitcast(dt.uint8)
+                else:
+                    s, t = T[sn + "s"][:, a:a + n], T[dn + "s"][:, b:b + n]
+                trs.append(RemoteDMATransfer(dst_ids=[DstId(rid=rid, pnc=pid)], dma_engine_mask=_bits(eng[d]),
+                                             remote_sem=T.sem[sem], srcs=[s], dsts=[t]))
+                sent[0] += len(eng[d])
+            g.remote_dma_fused(trs, local_sem=T.sem.sent)
+
+    def arriving(sender, dests):
+        return 2 * len(split(sender, dests)[core])
+
+    h = half(core)
+    own = 3 * HALF if h == 0 else 0
+
+    def slot(c, k):
+        return (2 - k) * HALF if half(c) == 0 else NC + k * HALF
+
+    def view(k):
+        if k < 0:
+            return own
+        return slot(core, k) if h == 0 else slot(core, k) - HALF
+
+    te = g.tensor
+
+    def decode(ps, t, v, start, stop, sem=None):
+        for b in range(4):
+            r = te.matmul_mx(ps[:, BANK * b:BANK * b + NC], T.sq[:, NC * b:NC * (b + 1)], T.sqs[:, NC * b:NC * (b + 1)],
+                             T[t][:, v:v + NC], T[t + "s"][:, v:v + NC], start, stop)
+            if sem:
+                r.then_inc(T.sem[sem + str(b)], 1)
+
+    if is_root:
+        g.sync.dma_start(T.b_sb[:], T.b[:]).then_inc(T.sem.ld_b, 16)
+        g.scalar.wait_ge(T.sem.ld_b, 16)
+    g.scalar.dma_start(T.a_sb[:], T.a[:]).then_inc(T.sem.ld_a, 16)
+
+    g.vector.memset(T.sel[:], 1.0).then_inc(T.sem.ones, 1)
+    g.wait_ge(T.sem.ones, 1)
+    g.affine_select(T.sel[:], T.sel[:], [[1, 516]], AluOpType.is_equal, 0.0, -3, -4).then_inc(T.sem.seld, 1)
+
+    if is_root:
+        g.vector.wait_ge(T.sem.ld_b, 16)
+        g.vector.quantize_mx(T.bq[:], T.bqs[:], T.b_sb[:]).then_inc(T.sem.bqd, 1)
+        b_there = 1
+    else:
+        up = [c for c in tree if core in tree[c]][0]
+        b_there = arriving(up, tree[up])
+    if core in tree:
+        g.wait_ge(T.sem.bqd, b_there)
+        send([(d, "bq", 0, NC, "bq", 0, "bqd") for d in tree[core]])
+
+    g.vector.memset(T.e2[:], 0.0).then_inc(T.sem.e2z, 1)
+    g.vector.wait_ge(T.sem.ld_a, 16)
+    g.vector.quantize_mx(T.aq[:], T.aqs[:], T.a_sb[:]).then_inc(T.sem.aqd, 1)
+    g.vector.wait_ge(T.sem.seld, 1)
+    for b in range(4):
+        g.vector.quantize_mx(T.sq[:, NC * b:NC * (b + 1)], T.sqs[:, NC * b:NC * (b + 1)],
+                             T.sel[:, 3 - b:3 - b + 512]).then_inc(T.sem.sqd, 1)
+
+    te.wait_ge(T.sem.aqd, 1)
+    te.wait_ge(T.sem.bqd, b_there)
+    for i in range(4):
+        te.matmul_mx(T.pt[:, BANK * i:BANK * i + NC], T.aq[:, NC * i:NC * (i + 1)], T.aqs[:, NC * i:NC * (i + 1)],
+                     T.bq[:], T.bqs[:], True, True).then_inc(T.sem["m%d" % i], 1)
+    te.wait_ge(T.sem.sqd, 4)
+    if is_agg:
+        te.wait_ge(T.sem.ing, arriving(root, [core]))
+        decode(T.ps, "gt", 0, True, True, "g")
+    e1 = T.e1f if is_agg else T.e1
+    for i in (0, 2):
+        g.vector.wait_ge(T.sem["m%d" % i], 1)
+        g.vector.tensor_scalar(e1[:, i:512:4], T.pt[:, BANK * i:BANK * i + NC], 0.0, None, AluOpType.max).then_inc(T.sem.rv, 1)
+    for i in (1, 3):
+        g.scalar.wait_ge(T.sem["m%d" % i], 1)
+        g.scalar.activation(e1[:, i:512:4], T.pt[:, BANK * i:BANK * i + NC], ActivationFunctionType.Relu).then_inc(T.sem.rs, 1)
+    g.vector.wait_ge(T.sem.rv, 2)
+    g.vector.wait_ge(T.sem.rs, 2)
+    if is_agg:
+        for i in range(4):
+            g.vector.wait_ge(T.sem["g%d" % i], 1)
+            g.vector.tensor_tensor(T.e1[:, i:512:4], T.e1f[:, i:512:4], T.ps[:, BANK * i:BANK * i + NC],
+                                   AluOpType.add).then_inc(T.sem.av, 1)
+        g.vector.wait_ge(T.sem.av, 4)
+    g.vector.quantize_mx(T.l1[:, own:own + NC], T.l1s[:, own:own + NC], T.e1[:]).then_inc(T.sem.qt, 1)
+
+    dests1 = lambda c: [near[c]["plane"], near[c]["plane_x"], near[c]["mate"]]
+    g.wait_ge(T.sem.qt, 1)
+    if is_root:
+        send([(me["mate"], "l1", own, NC, "gt", 0, "ing")])
+    else:
+        send([(d, "l1", own + HALF * half(d), HALF, "l1", slot(d, src[d].index(core)), "in%d" % src[d].index(core))
+              for d in dests1(core)])
+
+    te.wait_ge(T.sem.qt, 1)
+    last = len(src[core]) - 1
+    first = 0 if is_root else -1
+    for k in range(first, last + 1):
+        if k >= 0:
+            te.wait_ge(T.sem["in%d" % k], arriving(src[core][k], dests1(src[core][k])))
+        decode(T.ps, "l1", view(k), k == first, k == last, "d" if k == last else None)
+    at = 4 * HALF if h == 0 else 0
+    g.vector.wait_ge(T.sem.e2z, 1)
+    g.scalar.wait_ge(T.sem.e2z, 1)
+    for b in (0, 2):
+        g.vector.wait_ge(T.sem["d%d" % b], 1)
+        g.vector.tensor_copy(T.e2[:, at + b:at + 4 * HALF:4],
+                             T.ps[:, BANK * b + HALF * h:BANK * b + HALF * (h + 1)]).then_inc(T.sem.cv, 1)
+    for b in (1, 3):
+        g.scalar.wait_ge(T.sem["d%d" % b], 1)
+        g.scalar.activation(T.e2[:, at + b:at + 4 * HALF:4], T.ps[:, BANK * b + HALF * h:BANK * b + HALF * (h + 1)],
+                            ActivationFunctionType.Copy).then_inc(T.sem.cs, 1)
+    g.vector.wait_ge(T.sem.cv, 2)
+    g.vector.wait_ge(T.sem.cs, 2)
+    qo = 0 if h == 0 else HALF
+    g.vector.quantize_mx(T.qa[:, qo:qo + NC], T.qas[:, qo:qo + NC], T.e2[:]).then_inc(T.sem.qad, 1)
+
+    dests2 = lambda c: [near[c]["cable"], near[c]["cable_x"], near[c]["mate"]]
+    beside = 2 * HALF if half(me["mate"]) == 0 else 0
+    g.wait_ge(T.sem.qad, 1)
+    send([(me["cable"], "qa", HALF, HALF, "fb", HALF * h, "fb%d" % h),
+          (me["cable_x"], "qa", HALF, HALF, "fb", HALF * h, "fb%d" % h),
+          (me["mate"], "qa", HALF, HALF, "qa", beside, "fa")])
+
+    te.wait_ge(T.sem.qad, 1)
+    te.wait_ge(T.sem.fa, arriving(me["mate"], dests2(me["mate"])))
+    decode(T.pt, "qa", HALF if h == 0 else 0, True, False)
+    for d in (me["cable"], me["cable_x"]):
+        te.wait_ge(T.sem["fb%d" % half(d)], arriving(d, dests2(d)))
+    decode(T.pt, "fb", 0, False, True, "f")
+    for b in (0, 2):
+        g.vector.wait_ge(T.sem["f%d" % b], 1)
+        g.vector.tensor_copy(T.y_sb[:, b:512:4], T.pt[:, BANK * b:BANK * b + NC]).then_inc(T.sem.yv, 1)
+    for b in (1, 3):
+        g.scalar.wait_ge(T.sem["f%d" % b], 1)
+        g.scalar.activation(T.y_sb[:, b:512:4], T.pt[:, BANK * b:BANK * b + NC], ActivationFunctionType.Copy).then_inc(T.sem.ys, 1)
+
+    g.sync.wait_ge(T.sem.yv, 2)
+    g.sync.wait_ge(T.sem.ys, 2)
+    g.sync.dma_start(T.y[:], T.y_sb[:]).then_inc(T.sem.out, 16)
+    g.sync.wait_ge(T.sem.out, 16)
+    g.wait_ge(T.sem.sent, sent[0])

@@ -9,14 +9,15 @@ F8, U8 = "float8_e4m3fn_x4", "uint8"
 SCRATCH = {
     "a_sb": ("sbuf", [128, 2048], "bfloat16"),
     "b_sb": ("sbuf", [128, 512], "bfloat16"),
-    "sel": ("sbuf", [128, 516], "bfloat16"),
+    "sel": ("sbuf", [128, 772], "bfloat16"),
     "e1": ("sbuf", [128, 512], "bfloat16"),
     "e1f": ("sbuf", [128, 512], "float32"),
     "e2": ("sbuf", [128, 512], "bfloat16"),
     "y_sb": ("sbuf", [128, 512], "float32"),
     "aq": ("sbuf", [128, 512], F8), "aqs": ("sbuf", [128, 512], U8),
     "bq": ("sbuf", [128, 128], F8), "bqs": ("sbuf", [128, 128], U8),
-    "sq": ("sbuf", [128, 512], F8), "sqs": ("sbuf", [128, 512], U8),
+    "sq": ("sbuf", [128, 384], F8), "sqs": ("sbuf", [128, 384], U8),
+    "s3": ("sbuf", [128, 192], F8), "s3s": ("sbuf", [128, 192], U8),
     "gt": ("sbuf", [128, 128], F8), "gts": ("sbuf", [128, 128], U8),
     "l1": ("sbuf", [128, 320], F8), "l1s": ("sbuf", [128, 320], U8),
     "qa": ("sbuf", [128, 192], F8), "qas": ("sbuf", [128, 192], U8),
@@ -24,8 +25,8 @@ SCRATCH = {
     "pt": ("psum", [128, 2048], "float32"),
     "ps": ("psum", [128, 2048], "float32"),
 }
-SEMAPHORES = (["ld_a", "ld_b", "ones", "seld", "e2z", "aqd", "bqd", "sqd", "rv", "rs", "av", "qt", "cv", "cs", "qad", "yv", "ys",
-               "out", "sent", "ing", "fa", "fb0", "fb1", "in0", "in1", "in2"]
+SEMAPHORES = (["ld_a", "ld_b", "ones", "seld", "e2z", "aqd", "bqd", "bsd", "sqd", "s3q", "s3in", "rv", "rs", "av", "qt", "cv",
+               "cs", "qad", "yv", "ys", "out", "sent", "ing", "fa", "fb0", "fb1", "in0", "in1", "in2"]
               + [k + str(i) for k in "mgdf" for i in range(4)])
 
 
@@ -68,6 +69,7 @@ def rank_program(g, core, T, topo):
     near, root, tree, src = _plan(T, topo)
     me = near[core]
     is_root, is_agg = core == root, me["mate"] == root
+    shares = not (is_root or is_agg)
 
     def half(c):
         return topo.die(c)
@@ -79,28 +81,32 @@ def rank_program(g, core, T, topo):
         k = len(eng) // max(len(off), 1 if off else 2)
         out = {d: eng[i * k:(i + 1) * k] for i, d in enumerate(off)}
         if mate in dests:
-            out[mate] = [e for e in _engines(topo.mask(c, mate)) if e not in eng][:k]
+            rest = [e for e in _engines(topo.mask(c, mate)) if e not in eng]
+            out[mate] = rest[:k] if root in (c, mate) else rest
         return out
 
     sent = [0]
 
+    def put(eng, items, codes):
+        trs = []
+        for d, sn, a, n, dn, b, sem in items:
+            rid, pid = topo.addr(d, core)
+            if codes:
+                s, t = T[sn][:, a:a + n].bitcast(dt.uint8), T[dn][:, b:b + n].bitcast(dt.uint8)
+            else:
+                s, t = T[sn + "s"][:, a:a + n], T[dn + "s"][:, b:b + n]
+            trs.append(RemoteDMATransfer(dst_ids=[DstId(rid=rid, pnc=pid)], dma_engine_mask=_bits(eng[d]),
+                                         remote_sem=T.sem[sem], srcs=[s], dsts=[t]))
+            sent[0] += len(eng[d])
+        g.remote_dma_fused(trs, local_sem=T.sem.sent)
+
     def send(items):
         eng = split(core, [it[0] for it in items])
-        for codes in (True, False):
-            trs = []
-            for d, sn, a, n, dn, b, sem in items:
-                rid, pid = topo.addr(d, core)
-                if codes:
-                    s, t = T[sn][:, a:a + n].bitcast(dt.uint8), T[dn][:, b:b + n].bitcast(dt.uint8)
-                else:
-                    s, t = T[sn + "s"][:, a:a + n], T[dn + "s"][:, b:b + n]
-                trs.append(RemoteDMATransfer(dst_ids=[DstId(rid=rid, pnc=pid)], dma_engine_mask=_bits(eng[d]),
-                                             remote_sem=T.sem[sem], srcs=[s], dsts=[t]))
-                sent[0] += len(eng[d])
-            g.remote_dma_fused(trs, local_sem=T.sem.sent)
+        put(eng, items, True)
+        put(eng, items, False)
 
     def arriving(sender, dests):
-        return 2 * len(split(sender, dests)[core])
+        return len(split(sender, dests)[core])
 
     h = half(core)
     own = 3 * HALF if h == 0 else 0
@@ -113,12 +119,21 @@ def rank_program(g, core, T, topo):
             return own
         return slot(core, k) if h == 0 else slot(core, k) - HALF
 
+    qo = 0 if h == 0 else HALF
+    va = HALF if h == 0 else 0
+    beside = 2 * HALF if half(me["mate"]) == 0 else 0
+
     te = g.tensor
+
+    def selector(b):
+        if b == 3:
+            return T.s3[:, va:va + NC], T.s3s[:, va:va + NC]
+        return T.sq[:, NC * b:NC * (b + 1)], T.sqs[:, NC * b:NC * (b + 1)]
 
     def decode(ps, t, v, start, stop, sem=None):
         for b in range(4):
-            r = te.matmul_mx(ps[:, BANK * b:BANK * b + NC], T.sq[:, NC * b:NC * (b + 1)], T.sqs[:, NC * b:NC * (b + 1)],
-                             T[t][:, v:v + NC], T[t + "s"][:, v:v + NC], start, stop)
+            w, ws = selector(b)
+            r = te.matmul_mx(ps[:, BANK * b:BANK * b + NC], w, ws, T[t][:, v:v + NC], T[t + "s"][:, v:v + NC], start, stop)
             if sem:
                 r.then_inc(T.sem[sem + str(b)], 1)
 
@@ -127,37 +142,70 @@ def rank_program(g, core, T, topo):
         g.scalar.wait_ge(T.sem.ld_b, 16)
     g.scalar.dma_start(T.a_sb[:], T.a[:]).then_inc(T.sem.ld_a, 16)
 
-    g.vector.memset(T.sel[:], 1.0).then_inc(T.sem.ones, 1)
+    off, width = (256 if h == 0 else 0, 772) if shares else (0, 516)
+    g.vector.memset(T.sel[:, 0:width], 1.0).then_inc(T.sem.ones, 1)
     g.wait_ge(T.sem.ones, 1)
-    g.affine_select(T.sel[:], T.sel[:], [[1, 516]], AluOpType.is_equal, 0.0, -3, -4).then_inc(T.sem.seld, 1)
+    g.affine_select(T.sel[:, 0:width], T.sel[:, 0:width], [[1, width]], AluOpType.is_equal, 0.0,
+                    -3 - off, -4).then_inc(T.sem.seld, 1)
 
+    def make_selectors():
+        g.vector.wait_ge(T.sem.seld, 1)
+        if shares:
+            c0 = 0 if h == 0 else 256
+            g.vector.quantize_mx(T.s3[:, qo:qo + NC], T.s3s[:, qo:qo + NC], T.sel[:, c0:c0 + 512]).then_inc(T.sem.s3q, 1)
+        else:
+            g.vector.quantize_mx(T.s3[:, va:va + NC], T.s3s[:, va:va + NC], T.sel[:, off:off + 512]).then_inc(T.sem.s3q, 1)
+        for b in range(3):
+            g.vector.quantize_mx(T.sq[:, NC * b:NC * (b + 1)], T.sqs[:, NC * b:NC * (b + 1)],
+                                 T.sel[:, off + 3 - b:off + 3 - b + 512]).then_inc(T.sem.sqd, 1)
+
+    whole = lambda c: {near[c]["mate"]: _engines(topo.mask(c, near[c]["mate"]))}
+    if shares:
+        make_selectors()
+        g.wait_ge(T.sem.s3q, 1)
+        it = [(me["mate"], "s3", HALF, HALF, "s3", beside, "s3in")]
+        put(whole(core), it, True)
+        put(whole(core), it, False)
+
+    b_items = lambda l, codes: [(d, "bq", 0, NC, "bq", 0, "bqd" if codes else "bsd") for d in l]
     if is_root:
         g.vector.wait_ge(T.sem.ld_b, 16)
         g.vector.quantize_mx(T.bq[:], T.bqs[:], T.b_sb[:]).then_inc(T.sem.bqd, 1)
         b_there = 1
+        g.wait_ge(T.sem.bqd, 1)
+        eng = split(core, tree[core])
+        for l in ([d for d in tree[core] if d != me["mate"]], [me["mate"]]):
+            put(eng, b_items(l, False), False)
+            put(eng, b_items(l, True), True)
     else:
         up = [c for c in tree if core in tree[c]][0]
         b_there = arriving(up, tree[up])
-    if core in tree:
-        g.wait_ge(T.sem.bqd, b_there)
-        send([(d, "bq", 0, NC, "bq", 0, "bqd") for d in tree[core]])
+        if core in tree:
+            eng = split(core, tree[core])
+            g.wait_ge(T.sem.bsd, b_there)
+            put(eng, b_items(tree[core], False), False)
+            g.wait_ge(T.sem.bqd, b_there)
+            put(eng, b_items(tree[core], True), True)
 
     g.vector.memset(T.e2[:], 0.0).then_inc(T.sem.e2z, 1)
     g.vector.wait_ge(T.sem.ld_a, 16)
     g.vector.quantize_mx(T.aq[:], T.aqs[:], T.a_sb[:]).then_inc(T.sem.aqd, 1)
-    g.vector.wait_ge(T.sem.seld, 1)
-    for b in range(4):
-        g.vector.quantize_mx(T.sq[:, NC * b:NC * (b + 1)], T.sqs[:, NC * b:NC * (b + 1)],
-                             T.sel[:, 3 - b:3 - b + 512]).then_inc(T.sem.sqd, 1)
+    if not shares:
+        make_selectors()
 
     te.wait_ge(T.sem.aqd, 1)
+    if not is_root:
+        te.wait_ge(T.sem.bsd, b_there)
     te.wait_ge(T.sem.bqd, b_there)
     for i in range(4):
         te.matmul_mx(T.pt[:, BANK * i:BANK * i + NC], T.aq[:, NC * i:NC * (i + 1)], T.aqs[:, NC * i:NC * (i + 1)],
                      T.bq[:], T.bqs[:], True, True).then_inc(T.sem["m%d" % i], 1)
-    te.wait_ge(T.sem.sqd, 4)
+    te.wait_ge(T.sem.sqd, 3)
+    te.wait_ge(T.sem.s3q, 1)
+    if shares:
+        te.wait_ge(T.sem.s3in, 2 * len(whole(me["mate"])[core]))
     if is_agg:
-        te.wait_ge(T.sem.ing, arriving(root, [core]))
+        te.wait_ge(T.sem.ing, 2 * arriving(root, [core]))
         decode(T.ps, "gt", 0, True, True, "g")
     e1 = T.e1f if is_agg else T.e1
     for i in (0, 2):
@@ -189,7 +237,7 @@ def rank_program(g, core, T, topo):
     first = 0 if is_root else -1
     for k in range(first, last + 1):
         if k >= 0:
-            te.wait_ge(T.sem["in%d" % k], arriving(src[core][k], dests1(src[core][k])))
+            te.wait_ge(T.sem["in%d" % k], 2 * arriving(src[core][k], dests1(src[core][k])))
         decode(T.ps, "l1", view(k), k == first, k == last, "d" if k == last else None)
     at = 4 * HALF if h == 0 else 0
     g.vector.wait_ge(T.sem.e2z, 1)
@@ -204,21 +252,19 @@ def rank_program(g, core, T, topo):
                             ActivationFunctionType.Copy).then_inc(T.sem.cs, 1)
     g.vector.wait_ge(T.sem.cv, 2)
     g.vector.wait_ge(T.sem.cs, 2)
-    qo = 0 if h == 0 else HALF
     g.vector.quantize_mx(T.qa[:, qo:qo + NC], T.qas[:, qo:qo + NC], T.e2[:]).then_inc(T.sem.qad, 1)
 
     dests2 = lambda c: [near[c]["cable"], near[c]["cable_x"], near[c]["mate"]]
-    beside = 2 * HALF if half(me["mate"]) == 0 else 0
     g.wait_ge(T.sem.qad, 1)
     send([(me["cable"], "qa", HALF, HALF, "fb", HALF * h, "fb%d" % h),
           (me["cable_x"], "qa", HALF, HALF, "fb", HALF * h, "fb%d" % h),
           (me["mate"], "qa", HALF, HALF, "qa", beside, "fa")])
 
     te.wait_ge(T.sem.qad, 1)
-    te.wait_ge(T.sem.fa, arriving(me["mate"], dests2(me["mate"])))
-    decode(T.pt, "qa", HALF if h == 0 else 0, True, False)
+    te.wait_ge(T.sem.fa, 2 * arriving(me["mate"], dests2(me["mate"])))
+    decode(T.pt, "qa", va, True, False)
     for d in (me["cable"], me["cable_x"]):
-        te.wait_ge(T.sem["fb%d" % half(d)], arriving(d, dests2(d)))
+        te.wait_ge(T.sem["fb%d" % half(d)], 2 * arriving(d, dests2(d)))
     decode(T.pt, "fb", 0, False, True, "f")
     for b in (0, 2):
         g.vector.wait_ge(T.sem["f%d" % b], 1)

from concourse.bass import DstId, RemoteDMATransfer
from concourse.mybir import dt, AluOpType, ActivationFunctionType

NC = 128
HALF = NC // 2
BANK = 512

F8, U8 = "float8_e4m3fn_x4", "uint8"
SCRATCH = {
    "a_sb": ("sbuf", [128, 2048], "bfloat16"),
    "b_sb": ("sbuf", [128, 512], "bfloat16"),
    "sel": ("sbuf", [128, 772], "bfloat16"),
    "e1": ("sbuf", [128, 512], "bfloat16"),
    "e1f": ("sbuf", [128, 512], "float32"),
    "e2": ("sbuf", [128, 512], "bfloat16"),
    "y_sb": ("sbuf", [128, 512], "float32"),
    "aq": ("sbuf", [128, 512], F8), "aqs": ("sbuf", [128, 512], U8),
    "bq": ("sbuf", [128, 128], F8), "bqs": ("sbuf", [128, 128], U8),
    "sq": ("sbuf", [128, 384], F8), "sqs": ("sbuf", [128, 384], U8),
    "s3": ("sbuf", [128, 192], F8), "s3s": ("sbuf", [128, 192], U8),
    "gt": ("sbuf", [128, 128], F8), "gts": ("sbuf", [128, 128], U8),
    "l1": ("sbuf", [128, 320], F8), "l1s": ("sbuf", [128, 320], U8),
    "qa": ("sbuf", [128, 192], F8), "qas": ("sbuf", [128, 192], U8),
    "fb": ("sbuf", [128, 128], F8), "fbs": ("sbuf", [128, 128], U8),
    "pt": ("psum", [128, 2048], "float32"),
    "ps": ("psum", [128, 2048], "float32"),
}
SEMAPHORES = (["ld_a", "ld_b", "ones", "seld", "e2z", "aqd", "bqd", "bsd", "sqd", "s3q", "s3in", "rv", "rs", "av", "qt", "cv",
               "cs", "qad", "yv", "ys", "out", "sent", "ing", "fa", "fb0", "fb1", "in0", "in1", "in2"]
              + [k + str(i) for k in "mgdf" for i in range(4)])


def _engines(mask):
    return [e for e in range(16) if mask >> e & 1]


def _bits(engines):
    m = 0
    for e in engines:
        m |= 1 << e
    return m


def _plan(T, topo):
    cs = list(T.cores)
    pick = lambda l, c, same: [d for d in l if (topo.die(d) == topo.die(c)) == same][0]
    near = {}
    for c in cs:
        chip = [d for d in cs if d != c and topo.host(d) == topo.host(c) and topo.chip(d) == topo.chip(c)]
        plane = [d for d in cs if topo.same_plane(c, d)]
        cable = [d for d in cs if topo.rack(topo.host(d)) != topo.rack(topo.host(c)) and topo.may_write(c, d)]
        near[c] = {"mate": chip[0], "plane": pick(plane, c, True), "plane_x": pick(plane, c, False),
                   "cable": pick(cable, c, True), "cable_x": pick(cable, c, False)}
    root = cs[T.root]
    x, w = near[root]["cable"], near[root]["plane"]
    tree = {root: [x, w, near[root]["mate"]], x: [near[x]["plane"], near[x]["mate"]], w: [near[w]["cable_x"], near[w]["mate"]]}
    depth = {root: 0}
    for c in (root, x, w):
        for d in tree[c]:
            depth[d] = depth[c] + 1
    src = {c: sorted([d for d in (near[c]["mate"], near[c]["plane"], near[c]["plane_x"]) if d != root],
                     key=lambda d: depth[d]) for c in cs}
    return near, root, tree, src


def rank_program(g, core, T, topo):
    if T.rank_of(core) is None:
        return
    near, root, tree, src = _plan(T, topo)
    me = near[core]
    is_root, is_agg = core == root, me["mate"] == root
    shares = not (is_root or is_agg)

    def half(c):
        return topo.die(c)

    def split(c, dests):
        mate = near[c]["mate"]
        off = [d for d in dests if d != mate]
        eng = _engines(topo.mask(c, near[c]["plane"]))
        k = len(eng) // max(len(off), 1 if off else 2)
        out = {d: eng[i * k:(i + 1) * k] for i, d in enumerate(off)}
        if mate in dests:
            rest = [e for e in _engines(topo.mask(c, mate)) if e not in eng]
            out[mate] = rest[:k] if root in (c, mate) else rest
        return out

    sent = [0]

    def put(eng, items, codes):
        trs = []
        for d, sn, a, n, dn, b, sem in items:
            rid, pid = topo.addr(d, core)
            if codes:
                s, t = T[sn][:, a:a + n].bitcast(dt.uint8), T[dn][:, b:b + n].bitcast(dt.uint8)
            else:
                s, t = T[sn + "s"][:, a:a + n], T[dn + "s"][:, b:b + n]
            trs.append(RemoteDMATransfer(dst_ids=[DstId(rid=rid, pnc=pid)], dma_engine_mask=_bits(eng[d]),
                                         remote_sem=T.sem[sem], srcs=[s], dsts=[t]))
            sent[0] += len(eng[d])
        g.remote_dma_fused(trs, local_sem=T.sem.sent)

    def send(items):
        eng = split(core, [it[0] for it in items])
        put(eng, items, True)
        put(eng, items, False)

    def arriving(sender, dests):
        return len(split(sender, dests)[core])

    h = half(core)
    own = 3 * HALF if h == 0 else 0

    def slot(c, k):
        return (2 - k) * HALF if half(c) == 0 else NC + k * HALF

    def view(k):
        if k < 0:
            return own
        return slot(core, k) if h == 0 else slot(core, k) - HALF

    qo = 0 if h == 0 else HALF
    va = HALF if h == 0 else 0
    beside = 2 * HALF if half(me["mate"]) == 0 else 0

    te = g.tensor

    def selector(b):
        if b == 3:
            return T.s3[:, va:va + NC], T.s3s[:, va:va + NC]
        return T.sq[:, NC * b:NC * (b + 1)], T.sqs[:, NC * b:NC * (b + 1)]

    def decode(ps, t, v, start, stop, sem=None):
        for b in range(4):
            w, ws = selector(b)
            r = te.matmul_mx(ps[:, BANK * b:BANK * b + NC], w, ws, T[t][:, v:v + NC], T[t + "s"][:, v:v + NC], start, stop)
            if sem:
                r.then_inc(T.sem[sem + str(b)], 1)

    if is_root:
        g.sync.dma_start(T.b_sb[:], T.b[:]).then_inc(T.sem.ld_b, 16)
        g.scalar.wait_ge(T.sem.ld_b, 16)
    g.scalar.dma_start(T.a_sb[:], T.a[:]).then_inc(T.sem.ld_a, 16)

    off, width = (256 if h == 0 else 0, 772) if shares else (0, 516)
    g.vector.memset(T.sel[:, 0:width], 1.0).then_inc(T.sem.ones, 1)
    g.wait_ge(T.sem.ones, 1)
    g.affine_select(T.sel[:, 0:width], T.sel[:, 0:width], [[1, width]], AluOpType.is_equal, 0.0,
                    -3 - off, -4).then_inc(T.sem.seld, 1)

    def make_selectors():
        g.vector.wait_ge(T.sem.seld, 1)
        if shares:
            c0 = 0 if h == 0 else 256
            g.vector.quantize_mx(T.s3[:, qo:qo + NC], T.s3s[:, qo:qo + NC], T.sel[:, c0:c0 + 512]).then_inc(T.sem.s3q, 1)
        else:
            g.vector.quantize_mx(T.s3[:, va:va + NC], T.s3s[:, va:va + NC], T.sel[:, off:off + 512]).then_inc(T.sem.s3q, 1)
        for b in range(3):
            g.vector.quantize_mx(T.sq[:, NC * b:NC * (b + 1)], T.sqs[:, NC * b:NC * (b + 1)],
                                 T.sel[:, off + 3 - b:off + 3 - b + 512]).then_inc(T.sem.sqd, 1)

    whole = lambda c: {near[c]["mate"]: _engines(topo.mask(c, near[c]["mate"]))}
    if shares:
        make_selectors()
        g.wait_ge(T.sem.s3q, 1)
        it = [(me["mate"], "s3", HALF, HALF, "s3", beside, "s3in")]
        put(whole(core), it, True)
        put(whole(core), it, False)

    b_items = lambda l, codes: [(d, "bq", 0, NC, "bq", 0, "bqd" if codes else "bsd") for d in l]
    if is_root:
        g.vector.wait_ge(T.sem.ld_b, 16)
        g.vector.quantize_mx(T.bq[:], T.bqs[:], T.b_sb[:]).then_inc(T.sem.bqd, 1)
        b_there = 1
        g.wait_ge(T.sem.bqd, 1)
        eng = split(core, tree[core])
        for l in ([d for d in tree[core] if d != me["mate"]], [me["mate"]]):
            put(eng, b_items(l, False), False)
            put(eng, b_items(l, True), True)
    else:
        up = [c for c in tree if core in tree[c]][0]
        b_there = arriving(up, tree[up])
        if core in tree:
            eng = split(core, tree[core])
            g.wait_ge(T.sem.bsd, b_there)
            put(eng, b_items(tree[core], False), False)
            g.wait_ge(T.sem.bqd, b_there)
            put(eng, b_items(tree[core], True), True)

    g.vector.memset(T.e2[:], 0.0).then_inc(T.sem.e2z, 1)
    g.vector.wait_ge(T.sem.ld_a, 16)
    g.vector.quantize_mx(T.aq[:], T.aqs[:], T.a_sb[:]).then_inc(T.sem.aqd, 1)
    if not shares:
        make_selectors()

    te.wait_ge(T.sem.aqd, 1)
    if not is_root:
        te.wait_ge(T.sem.bsd, b_there)
    te.wait_ge(T.sem.bqd, b_there)
    for i in range(4):
        te.matmul_mx(T.pt[:, BANK * i:BANK * i + NC], T.aq[:, NC * i:NC * (i + 1)], T.aqs[:, NC * i:NC * (i + 1)],
                     T.bq[:], T.bqs[:], True, True).then_inc(T.sem["m%d" % i], 1)
    te.wait_ge(T.sem.sqd, 3)
    te.wait_ge(T.sem.s3q, 1)
    if shares:
        te.wait_ge(T.sem.s3in, 2 * len(whole(me["mate"])[core]))
    if is_agg:
        te.wait_ge(T.sem.ing, 2 * arriving(root, [core]))
        decode(T.ps, "gt", 0, True, True, "g")
    e1 = T.e1f if is_agg else T.e1
    for i in (0, 2):
        g.vector.wait_ge(T.sem["m%d" % i], 1)
        g.vector.tensor_scalar(e1[:, i:512:4], T.pt[:, BANK * i:BANK * i + NC], 0.0, None, AluOpType.max).then_inc(T.sem.rv, 1)
    for i in (1, 3):
        g.scalar.wait_ge(T.sem["m%d" % i], 1)
        g.scalar.activation(e1[:, i:512:4], T.pt[:, BANK * i:BANK * i + NC], ActivationFunctionType.Relu).then_inc(T.sem.rs, 1)
    g.vector.wait_ge(T.sem.rv, 2)
    g.vector.wait_ge(T.sem.rs, 2)
    if is_agg:
        for i in range(4):
            g.vector.wait_ge(T.sem["g%d" % i], 1)
            g.vector.tensor_tensor(T.e1[:, i:512:4], T.e1f[:, i:512:4], T.ps[:, BANK * i:BANK * i + NC],
                                   AluOpType.add).then_inc(T.sem.av, 1)
        g.vector.wait_ge(T.sem.av, 4)
    g.vector.quantize_mx(T.l1[:, own:own + NC], T.l1s[:, own:own + NC], T.e1[:]).then_inc(T.sem.qt, 1)

    dests1 = lambda c: [near[c]["plane"], near[c]["plane_x"], near[c]["mate"]]
    g.wait_ge(T.sem.qt, 1)
    if is_root:
        send([(me["mate"], "l1", own, NC, "gt", 0, "ing")])
    else:
        send([(d, "l1", own + HALF * half(d), HALF, "l1", slot(d, src[d].index(core)), "in%d" % src[d].index(core))
              for d in dests1(core)])

    te.wait_ge(T.sem.qt, 1)
    last = len(src[core]) - 1
    first = 0 if is_root else -1
    for k in range(first, last + 1):
        if k >= 0:
            te.wait_ge(T.sem["in%d" % k], 2 * arriving(src[core][k], dests1(src[core][k])))
        decode(T.ps, "l1", view(k), k == first, k == last, "d" if k == last else None)
    at = 4 * HALF if h == 0 else 0
    g.vector.wait_ge(T.sem.e2z, 1)
    g.scalar.wait_ge(T.sem.e2z, 1)
    for b in (0, 2):
        g.vector.wait_ge(T.sem["d%d" % b], 1)
        g.vector.tensor_copy(T.e2[:, at + b:at + 4 * HALF:4],
                             T.ps[:, BANK * b + HALF * h:BANK * b + HALF * (h + 1)]).then_inc(T.sem.cv, 1)
    for b in (1, 3):
        g.scalar.wait_ge(T.sem["d%d" % b], 1)
        g.scalar.activation(T.e2[:, at + b:at + 4 * HALF:4], T.ps[:, BANK * b + HALF * h:BANK * b + HALF * (h + 1)],
                            ActivationFunctionType.Copy).then_inc(T.sem.cs, 1)
    g.vector.wait_ge(T.sem.cv, 2)
    g.vector.wait_ge(T.sem.cs, 2)
    g.vector.quantize_mx(T.qa[:, qo:qo + NC], T.qas[:, qo:qo + NC], T.e2[:]).then_inc(T.sem.qad, 1)

    dests2 = lambda c: [near[c]["cable"], near[c]["cable_x"], near[c]["mate"]]
    g.wait_ge(T.sem.qad, 1)
    send([(me["cable"], "qa", HALF, HALF, "fb", HALF * h, "fb%d" % h),
          (me["cable_x"], "qa", HALF, HALF, "fb", HALF * h, "fb%d" % h),
          (me["mate"], "qa", HALF, HALF, "qa", beside, "fa")])

    te.wait_ge(T.sem.qad, 1)
    te.wait_ge(T.sem.fa, 2 * arriving(me["mate"], dests2(me["mate"])))
    decode(T.pt, "qa", va, True, False)
    for d in (me["cable"], me["cable_x"]):
        te.wait_ge(T.sem["fb%d" % half(d)], 2 * arriving(d, dests2(d)))
    decode(T.pt, "fb", 0, False, True, "f")
    for b in (0, 2):
        g.vector.wait_ge(T.sem["f%d" % b], 1)
        g.vector.tensor_copy(T.y_sb[:, b:512:4], T.pt[:, BANK * b:BANK * b + NC]).then_inc(T.sem.yv, 1)
    for b in (1, 3):
        g.scalar.wait_ge(T.sem["f%d" % b], 1)
        g.scalar.activation(T.y_sb[:, b:512:4], T.pt[:, BANK * b:BANK * b + NC], ActivationFunctionType.Copy).then_inc(T.sem.ys, 1)

    g.sync.wait_ge(T.sem.yv, 2)
    g.sync.wait_ge(T.sem.ys, 2)
    g.sync.dma_start(T.y[:], T.y_sb[:]).then_inc(T.sem.out, 16)
    g.sync.wait_ge(T.sem.out, 16)
    g.wait_ge(T.sem.sent, sent[0])
